import numpy as np
import ml_dtypes


def mxq(x, axis, fmt="e4m3"):
    dtype, down = {"e4m3": (ml_dtypes.float8_e4m3fn, 7), "e5m2": (ml_dtypes.float8_e5m2, 14)}[fmt]
    v = np.moveaxis(np.asarray(x, np.float32).astype(ml_dtypes.bfloat16).astype(np.float64), axis, -1)
    blocks = v.reshape(v.shape[:-1] + (-1, 32))
    amax = np.abs(blocks).max(-1, keepdims=True)
    byte = np.maximum(np.where(amax > 0, np.frexp(amax)[1] - 1 + 127, 0) - down, 1)
    scale = np.exp2(byte - 127.0)
    codes = (blocks / scale).astype(np.float32).astype(dtype).astype(np.float64)
    return np.moveaxis((codes * scale).reshape(v.shape), -1, axis)


WIDE = False


def mx_kscale(k):
    if not WIDE:
        return np.ones(k)
    levels = np.array([10, -10, 5, -5, 0])
    if k % 512:
        return np.exp2(np.random.permutation(np.resize(levels, k // 32))).repeat(32)
    a = np.empty((k // 512, 16))
    for p in range(k // 512):
        a[p, :8] = np.random.permutation(np.resize(levels, 8))
        for g in range(8):
            far = levels[np.abs(levels - a[p, g]) >= 10]
            a[p, g + 8] = far[np.random.randint(len(far))]
    return np.exp2(a.ravel()).repeat(32)


def f64(x):
    return np.asarray(x).astype(np.float64)


def striped(idx):
    return np.tile(idx.reshape(-1, 16).T, (8, 1)).astype(np.uint16)


def unstriped(offs):
    return offs[:16].T.reshape(-1).astype(np.int64)


def pack_weight(w):
    k, n = w.shape
    w = f64(np.asarray(w, np.float32).astype(ml_dtypes.bfloat16)).reshape(k // 32, 32, n)
    amax = np.abs(w).max(1)
    byte = np.clip(np.where(amax > 0, np.frexp(amax)[1] - 1 + 127 - 7, 1), 1, 254)
    scaled = (w * np.exp2(127.0 - byte)[:, None, :]).reshape(k, n).astype(np.float32)
    words = np.ascontiguousarray(scaled.reshape(k // 512, 128, 4, n).transpose(0, 1, 3, 2)).astype(ml_dtypes.float8_e4m3fn).view(np.uint8)
    return words, np.ascontiguousarray(byte.astype(np.uint8).reshape(k // 512, 16, n))


def unpack_weight(words, scales):
    g, p, n, _ = words.shape
    vals = np.ascontiguousarray(words).view(ml_dtypes.float8_e4m3fn).astype(np.float64) * np.repeat(np.exp2(scales.astype(np.float64) - 127.0), 8, axis=1)[..., None]
    return vals.transpose(0, 1, 3, 2).reshape(g * 512, n)


K, T, S, N, U = 512, 2048, 512, 256, 1024


def setup_inputs():
    n = np.random.standard_normal
    s = mx_kscale(K)[:, None]
    packed_xT = pack_weight(n((K, T)) * s)
    return {
        "x_words": packed_xT[0],
        "x_scales": packed_xT[1],
        "w1": (n((K, N)) / np.sqrt(K) / s).astype(np.float32),
        "w2": (n((K, N)) / np.sqrt(K) / s).astype(np.float32),
        "w3": (n((K, N)) / np.sqrt(K) / s).astype(np.float32),
        "qm": (np.random.uniform(0.3, 0.8, (N, 1))).astype(np.float32),
        "velx": (n((N, U))).astype(np.float32),
        "vely": (n((N, U))).astype(np.float32),
        "offs": striped(np.random.permutation(T)[:S]),
        "cell": striped(np.random.permutation(np.concatenate([np.arange(S), np.random.randint(0, S, U - S)]))),
    }


def reference(x_words, x_scales, w1, w2, w3, qm, velx, vely, offs, cell):
    xq = unpack_weight(x_words, x_scales)[:, unstriped(offs)]
    ex = mxq(f64(w1), 0, "e4m3").T @ xq
    gx = ex[:, unstriped(cell)]
    ax = f64(qm) * gx
    vx = f64(velx) + ax
    ey = mxq(f64(w2), 0, "e4m3").T @ xq
    gy = ey[:, unstriped(cell)]
    ay = f64(qm) * gy
    vy = f64(vely) + ay
    bz = mxq(f64(w3), 0, "e4m3").T @ xq
    tz = bz[:, unstriped(cell)]
    tw = f64(qm) * tz
    wy = vy - (vx * tw)
    sw = (2.0 * tw) / ((tw) ** 2 + 1.0)
    return vx + wy * sw + ax

@@ -1,0 +1,222 @@
+from contextlib import ExitStack
+
+import concourse.mybir as mybir
+
+K, T, S, N, U = 512, 2048, 512, 256, 1024
+FLOPS = 3 * 2 * K * N * S
+
+F32 = mybir.dt.float32
+BF16 = mybir.dt.bfloat16
+I32 = mybir.dt.int32
+U32 = mybir.dt.uint32
+U16 = mybir.dt.uint16
+U8 = mybir.dt.uint8
+FP8X4 = mybir.dt.float8_e4m3fn_x4
+ALU = mybir.AluOpType
+ACT = mybir.ActivationFunctionType
+
+P = 128
+PACK = 4
+BLOCKS = N // P
+HALF = 512
+HALVES = U // HALF
+WIN = S + 32
+LOG_WIN = 2 * S
+
+
+def tile_picked_yboris_vel_p_kernel(tc, x_words, x_scales, w1, w2, w3, qm, velx, vely, offs, cell, out):
+    nc = tc.nc
+    with ExitStack() as ctx:
+        keep = ctx.enter_context(tc.tile_pool(name="keep", bufs=1))
+        psum = ctx.enter_context(tc.psum_pool(name="psum", bufs=1))
+
+        offs_t = keep.tile([P, S // 16], U16, name="offs_t")
+        cell_t = keep.tile([P, U // 16], U16, name="cell_t")
+        words = keep.tile([P, T], I32, name="words", align_bytes=64)
+        planes = keep.tile([P, T], U8, name="planes", align_bytes=64)
+        x_codes = [keep.tile([P, S // 2], U32, name=f"x_codes{c}", align_bytes=64) for c in range(2)]
+        x_plane = keep.tile([P, S], U8, name="x_plane", align_bytes=64)
+        qm_t = keep.tile([P, BLOCKS], F32, name="qm_t")
+        one = keep.tile([P, 8], F32, name="one")
+        warm = keep.tile([P, 8], F32, name="warm")
+
+        weights = {"ex": w1, "ey": w2, "bz": w3}
+        raw, grouped, codes, scales, acc = {}, {}, {}, {}, {}
+        for name in weights:
+            for b in range(BLOCKS):
+                raw[name, b] = keep.tile([P, PACK, P], F32, name=f"raw_{name}{b}")
+                grouped[name, b] = keep.tile([P, P, PACK], BF16, name=f"grouped_{name}{b}", align_bytes=64)
+                codes[name, b] = keep.tile([P, P], U32, name=f"codes_{name}{b}", align_bytes=64)
+                scales[name, b] = keep.tile([P, P], U8, name=f"scales_{name}{b}", align_bytes=64)
+                acc[name, b] = psum.tile([P, S], F32, name=f"acc_{name}{b}")
+
+        spare_bank = psum.tile([P, S], F32, name="spare_bank")
+
+        def per_block(name, width):
+            return [keep.tile([P, width], F32, name=f"{name}{b}") for b in range(BLOCKS)]
+
+        def per_half(name):
+            return {(b, h): keep.tile([P, HALF], F32, name=f"{name}{b}{h}") for b in range(BLOCKS) for h in range(HALVES)}
+
+        vx, vy = per_half("vx"), per_half("vy")
+        tw, kick, logs = per_block("tw", WIN), per_block("kick", LOG_WIN), per_block("logs", LOG_WIN)
+        u1, u2, u3, u4, gain, res = (per_half(n) for n in ("u1", "u2", "u3", "u4", "gain", "res"))
+
+        def load_w(name, b):
+            nc.sync.dma_start(out=raw[name, b][:], in_=weights[name][:, b * P : (b + 1) * P].rearrange("(p j) m -> p j m", j=PACK))
+
+        def cast_w(name, b, copy=nc.scalar.copy):
+            copy(
+                out=grouped[name, b][:].rearrange("p (c i) j -> p c j i", i=4),
+                in_=raw[name, b][:].rearrange("p j (c i) -> p c j i", i=4),
+            )
+
+        def quant_w(name, b):
+            nc.vector.quantize_mx(
+                out=codes[name, b][:].bitcast(FP8X4), scales=scales[name, b][:], in_=grouped[name, b][:].rearrange("p m j -> p (m j)")
+            )
+
+        def product(name, b):
+            for c in range(2):
+                half_product(acc[name, b][:, cells_of(c)], name, b, c)
+
+        def cells_of(c):
+            return slice(c * S // 2, (c + 1) * S // 2)
+
+        def half_product(dst, name, b, c):
+            nc.tensor.matmul_mx(
+                out=dst,
+                lhsT=codes[name, b][:].bitcast(FP8X4),
+                lhsT_scale=scales[name, b][:],
+                rhs=x_codes[c][:].bitcast(FP8X4),
+                rhs_scale=x_plane[:, cells_of(c)],
+                start=True,
+                stop=True,
+            )
+
+        def picks(h):
+            return cell_t[:, h * HALF // 16 : (h + 1) * HALF // 16]
+
+        def cols_of(h):
+            return slice(h * HALF, (h + 1) * HALF)
+
+        nc.vector.memset(planes[:].bitcast(I32), 0)
+        nc.vector.memset(one[:], 1.0)
+        for b in range(BLOCKS):
+            nc.vector.memset(tw[b][:, S:], 0.0)
+
+        def load_scales(queue, q):
+            queue.dma_start(out=planes[32 * q : 32 * q + 4, :].bitcast(I32), in_=x_scales[0, 4 * q : 4 * q + 4, :].bitcast(I32))
+
+        def load_vel(tiles, src, b, h):
+            nc.sync.dma_start(out=tiles[b, h][:], in_=src[b * P : (b + 1) * P, cols_of(h)])
+
+        load_w("bz", 0)
+        nc.sync.dma_start(offs_t[:], offs)
+        for q in range(4):
+            load_scales(nc.sync, q)
+        nc.scalar.activation(warm[:], one[:], ACT.Ln)
+        nc.sync.dma_start(out=words[:], in_=x_words[0].rearrange("p c r -> p (c r)").bitcast(I32))
+        with nc.allow_non_contiguous_dma(reason="one value of qm a partition and block"):
+            nc.sync.dma_start(out=qm_t[:], in_=qm.rearrange("(b p) o -> p (b o)", p=P))
+        nc.sync.dma_start(cell_t[:], cell)
+        load_w("bz", 1)
+        load_w("ey", 0)
+        load_vel(vy, vely, 0, 0)
+        load_w("ex", 0)
+        load_vel(vy, vely, 0, 1)
+        load_vel(vx, velx, 0, 0)
+        load_vel(vx, velx, 0, 1)
+        load_w("ey", 1)
+        load_w("ex", 1)
+        for h in range(HALVES):
+            load_vel(vy, vely, 1, h)
+        for h in range(HALVES):
+            load_vel(vx, velx, 1, h)
+
+        nc.vector.tensor_copy(x_plane[:], planes[:].indirect(offs_t[:]))
+        cast_w("bz", 0)
+        quant_w("bz", 0)
+        for c in range(2):
+            nc.vector.tensor_copy(x_codes[c][:], words[:].bitcast(U32).indirect(offs_t[:, c * S // 32 : (c + 1) * S // 32]))
+            bank = acc["bz", 0] if c == 0 else spare_bank
+            half_product(bank[:, cells_of(c)], "bz", 0, c)
+            nc.scalar.activation(tw[0][:, cells_of(c)], bank[:, cells_of(c)], ACT.Copy, scale=qm_t[:, 0:1])
+
+        def rotate_term(b, h):
+            nc.vector.tensor_tensor(u1[b, h][:], tw[b][:].indirect(picks(h)), vy[b, h][:], ALU.mult)
+
+        def square(b):
+            nc.scalar.activation(logs[1 - b][:, S:], tw[b][:, :S], ACT.Square)
+
+        def log_gain(b):
+            nc.scalar.activation(logs[b][:, :S], logs[1 - b][:, S:], ACT.Ln, bias=2.0**-60)
+
+        def kick_y(b):
+            nc.vector.scalar_tensor_tensor(kick[b][:, S:], acc["ey", b][:], qm_t[:, b : b + 1], tw[b][:, :S], ALU.mult, ALU.mult)
+
+        def kick_x(b):
+            nc.vector.scalar_tensor_tensor(kick[b][:, :S], acc["ex", b][:], qm_t[:, b : b + 1], kick[b][:, S:], ALU.mult, ALU.add)
+
+        def fetch_gain(b):
+            for h in range(HALVES):
+                nc.scalar.activation(gain[b, h][:], logs[b][:].indirect(picks(h)), ACT.Sigmoid, scale=-1.0)
+
+        def add_kick(b, h):
+            nc.vector.tensor_tensor(u2[b, h][:], kick[b][:].indirect(picks(h)), u1[b, h][:], ALU.add)
+
+        def add_vx(b, h):
+            nc.vector.tensor_tensor(u3[b, h][:], u2[b, h][:], vx[b, h][:], ALU.add)
+
+        def rotate(b, h):
+            nc.vector.tensor_tensor(u4[b, h][:], u3[b, h][:], gain[b, h][:], ALU.mult)
+
+        def finish(b, h):
+            nc.vector.scalar_tensor_tensor(res[b, h][:], u4[b, h][:], 2.0, vx[b, h][:], ALU.mult, ALU.subtract)
+            nc.sync.dma_start(out=out[b * P : (b + 1) * P, cols_of(h)], in_=res[b, h][:])
+
+        cast_w("bz", 1, nc.vector.tensor_copy)
+        cast_w("ey", 0, nc.vector.tensor_copy)
+        for name, b in (("bz", 1), ("ey", 0)):
+            quant_w(name, b)
+            product(name, b)
+        cast_w("ex", 0)
+        nc.scalar.activation(tw[1][:, :S], acc["bz", 1][:], ACT.Copy, scale=qm_t[:, 1:2])
+        for b in range(BLOCKS):
+            square(b)
+        for b in range(BLOCKS):
+            log_gain(b)
+        rotate_term(0, 0)
+        quant_w("ex", 0)
+        product("ex", 0)
+        kick_y(0)
+        rotate_term(0, 1)
+        kick_x(0)
+        cast_w("ey", 1)
+        cast_w("ex", 1)
+        fetch_gain(0)
+        fetch_gain(1)
+        quant_w("ey", 1)
+        product("ey", 1)
+        add_kick(0, 0)
+        quant_w("ex", 1)
+        product("ex", 1)
+        add_kick(0, 1)
+        add_vx(0, 0)
+        kick_y(1)
+        add_vx(0, 1)
+        kick_x(1)
+        rotate(0, 0)
+        rotate(0, 1)
+        finish(0, 0)
+        finish(0, 1)
+        rotate_term(1, 0)
+        rotate_term(1, 1)
+        add_kick(1, 0)
+        add_kick(1, 1)
+        add_vx(1, 0)
+        add_vx(1, 1)
+        rotate(1, 0)
+        rotate(1, 1)
+        finish(1, 0)
+        finish(1, 1)

@@ -1,6 +1,7 @@
 from contextlib import ExitStack
 
 import concourse.mybir as mybir
+from concourse.masks import make_identity
 
 K, T, S, N, U = 512, 2048, 512, 256, 1024
 FLOPS = 3 * 2 * K * N * S
@@ -18,10 +19,9 @@ ACT = mybir.ActivationFunctionType
 P = 128
 PACK = 4
 BLOCKS = N // P
-HALF = 512
-HALVES = U // HALF
-WIN = S + 32
-LOG_WIN = 2 * S
+HALF = U // 2
+SPARE = 32
+TINY = 2.0**-60
 
 
 def tile_picked_yboris_vel_p_kernel(tc, x_words, x_scales, w1, w2, w3, qm, velx, vely, offs, cell, out):
@@ -39,36 +39,55 @@ def tile_picked_yboris_vel_p_kernel(tc, x_words, x_scales, w1, w2, w3, qm, velx,
         qm_t = keep.tile([P, BLOCKS], F32, name="qm_t")
         one = keep.tile([P, 8], F32, name="one")
         warm = keep.tile([P, 8], F32, name="warm")
+        ident = keep.tile([P, P], F32, name="ident")
 
         weights = {"ex": w1, "ey": w2, "bz": w3}
         raw, grouped, codes, scales, acc = {}, {}, {}, {}, {}
         for name in weights:
+            raw[name] = keep.tile([P, PACK, N], F32, name=f"raw_{name}")
             for b in range(BLOCKS):
-                raw[name, b] = keep.tile([P, PACK, P], F32, name=f"raw_{name}{b}")
                 grouped[name, b] = keep.tile([P, P, PACK], BF16, name=f"grouped_{name}{b}", align_bytes=64)
                 codes[name, b] = keep.tile([P, P], U32, name=f"codes_{name}{b}", align_bytes=64)
                 scales[name, b] = keep.tile([P, P], U8, name=f"scales_{name}{b}", align_bytes=64)
-                acc[name, b] = psum.tile([P, S], F32, name=f"acc_{name}{b}")
-
-        spare_bank = psum.tile([P, S], F32, name="spare_bank")
+                acc[name, b] = psum.tile([P, S], F32, name=f"acc_{name}{b}", tag=f"acc_{name}{b}")
+        second_bank = psum.tile([P, S], F32, name="second_bank", tag="second_bank")
 
         def per_block(name, width):
             return [keep.tile([P, width], F32, name=f"{name}{b}") for b in range(BLOCKS)]
 
-        def per_half(name):
-            return {(b, h): keep.tile([P, HALF], F32, name=f"{name}{b}{h}") for b in range(BLOCKS) for h in range(HALVES)}
+        def per_half(name, skip=()):
+            return {
+                (b, h): keep.tile([P, HALF], F32, name=f"{name}{b}{h}") for b in range(BLOCKS) for h in range(2) if (b, h) not in skip
+            }
 
         vx, vy = per_half("vx"), per_half("vy")
-        tw, kick, logs = per_block("tw", WIN), per_block("kick", LOG_WIN), per_block("logs", LOG_WIN)
-        u1, u2, u3, u4, gain, res = (per_half(n) for n in ("u1", "u2", "u3", "u4", "gain", "res"))
+        tw, kick, logs = per_block("tw", S + SPARE), per_block("kick", 2 * S), per_block("logs", 2 * S)
+        cross, inner, gain = per_half("cross", [(1, 0), (1, 1)]), per_half("inner", [(1, 0)]), per_half("gain", [(1, 1)])
+        kept, turned, res = per_half("kept"), per_half("turned"), per_half("res")
+        cross[1, 0] = cross[0, 1]
+        inner[1, 0] = inner[0, 1]
+        cross[1, 1] = inner[1, 0]
+        gain[1, 1] = gain[0, 0]
 
-        def load_w(name, b):
-            nc.sync.dma_start(out=raw[name, b][:], in_=weights[name][:, b * P : (b + 1) * P].rearrange("(p j) m -> p j m", j=PACK))
+        def rows_of(b):
+            return slice(b * P, (b + 1) * P)
 
-        def cast_w(name, b, copy=nc.scalar.copy):
+        def cells_of(c):
+            return slice(c * S // 2, (c + 1) * S // 2)
+
+        def picks(first, count):
+            return cell_t[:, first // 16 : (first + count) // 16]
+
+        def load_w(name):
+            nc.sync.dma_start(out=raw[name][:], in_=weights[name].rearrange("(p j) m -> p j m", j=PACK))
+
+        def load_vel(tiles, src, b, h):
+            nc.sync.dma_start(out=tiles[b, h][:], in_=src[rows_of(b), h * HALF : (h + 1) * HALF])
+
+        def cast_w(name, b, copy):
             copy(
                 out=grouped[name, b][:].rearrange("p (c i) j -> p c j i", i=4),
-                in_=raw[name, b][:].rearrange("p j (c i) -> p c j i", i=4),
+                in_=raw[name][:, :, rows_of(b)].rearrange("p j (c i) -> p c j i", i=4),
             )
 
         def quant_w(name, b):
@@ -76,16 +95,9 @@ def tile_picked_yboris_vel_p_kernel(tc, x_words, x_scales, w1, w2, w3, qm, velx,
                 out=codes[name, b][:].bitcast(FP8X4), scales=scales[name, b][:], in_=grouped[name, b][:].rearrange("p m j -> p (m j)")
             )
 
-        def product(name, b):
-            for c in range(2):
-                half_product(acc[name, b][:, cells_of(c)], name, b, c)
-
-        def cells_of(c):
-            return slice(c * S // 2, (c + 1) * S // 2)
-
-        def half_product(dst, name, b, c):
+        def half_product(bank, name, b, c):
             nc.tensor.matmul_mx(
-                out=dst,
+                out=bank[:, cells_of(c)],
                 lhsT=codes[name, b][:].bitcast(FP8X4),
                 lhsT_scale=scales[name, b][:],
                 rhs=x_codes[c][:].bitcast(FP8X4),
@@ -94,63 +106,9 @@ def tile_picked_yboris_vel_p_kernel(tc, x_words, x_scales, w1, w2, w3, qm, velx,
                 stop=True,
             )
 
-        def picks(h):
-            return cell_t[:, h * HALF // 16 : (h + 1) * HALF // 16]
-
-        def cols_of(h):
-            return slice(h * HALF, (h + 1) * HALF)
-
-        nc.vector.memset(planes[:].bitcast(I32), 0)
-        nc.vector.memset(one[:], 1.0)
-        for b in range(BLOCKS):
-            nc.vector.memset(tw[b][:, S:], 0.0)
-
-        def load_scales(queue, q):
-            queue.dma_start(out=planes[32 * q : 32 * q + 4, :].bitcast(I32), in_=x_scales[0, 4 * q : 4 * q + 4, :].bitcast(I32))
-
-        def load_vel(tiles, src, b, h):
-            nc.sync.dma_start(out=tiles[b, h][:], in_=src[b * P : (b + 1) * P, cols_of(h)])
-
-        load_w("bz", 0)
-        nc.sync.dma_start(offs_t[:], offs)
-        for q in range(4):
-            load_scales(nc.sync, q)
-        nc.scalar.activation(warm[:], one[:], ACT.Ln)
-        nc.sync.dma_start(out=words[:], in_=x_words[0].rearrange("p c r -> p (c r)").bitcast(I32))
-        with nc.allow_non_contiguous_dma(reason="one value of qm a partition and block"):
-            nc.sync.dma_start(out=qm_t[:], in_=qm.rearrange("(b p) o -> p (b o)", p=P))
-        nc.sync.dma_start(cell_t[:], cell)
-        load_w("bz", 1)
-        load_w("ey", 0)
-        load_vel(vy, vely, 0, 0)
-        load_w("ex", 0)
-        load_vel(vy, vely, 0, 1)
-        load_vel(vx, velx, 0, 0)
-        load_vel(vx, velx, 0, 1)
-        load_w("ey", 1)
-        load_w("ex", 1)
-        for h in range(HALVES):
-            load_vel(vy, vely, 1, h)
-        for h in range(HALVES):
-            load_vel(vx, velx, 1, h)
-
-        nc.vector.tensor_copy(x_plane[:], planes[:].indirect(offs_t[:]))
-        cast_w("bz", 0)
-        quant_w("bz", 0)
-        for c in range(2):
-            nc.vector.tensor_copy(x_codes[c][:], words[:].bitcast(U32).indirect(offs_t[:, c * S // 32 : (c + 1) * S // 32]))
-            bank = acc["bz", 0] if c == 0 else spare_bank
-            half_product(bank[:, cells_of(c)], "bz", 0, c)
-            nc.scalar.activation(tw[0][:, cells_of(c)], bank[:, cells_of(c)], ACT.Copy, scale=qm_t[:, 0:1])
-
-        def rotate_term(b, h):
-            nc.vector.tensor_tensor(u1[b, h][:], tw[b][:].indirect(picks(h)), vy[b, h][:], ALU.mult)
-
-        def square(b):
-            nc.scalar.activation(logs[1 - b][:, S:], tw[b][:, :S], ACT.Square)
-
-        def log_gain(b):
-            nc.scalar.activation(logs[b][:, :S], logs[1 - b][:, S:], ACT.Ln, bias=2.0**-60)
+        def product(name, b):
+            for c in range(2):
+                half_product(acc[name, b], name, b, c)
 
         def kick_y(b):
             nc.vector.scalar_tensor_tensor(kick[b][:, S:], acc["ey", b][:], qm_t[:, b : b + 1], tw[b][:, :S], ALU.mult, ALU.mult)
@@ -158,65 +116,124 @@ def tile_picked_yboris_vel_p_kernel(tc, x_words, x_scales, w1, w2, w3, qm, velx,
         def kick_x(b):
             nc.vector.scalar_tensor_tensor(kick[b][:, :S], acc["ex", b][:], qm_t[:, b : b + 1], kick[b][:, S:], ALU.mult, ALU.add)
 
-        def fetch_gain(b):
-            for h in range(HALVES):
-                nc.scalar.activation(gain[b, h][:], logs[b][:].indirect(picks(h)), ACT.Sigmoid, scale=-1.0)
+        def fetch_gain(b, h):
+            nc.scalar.activation(gain[b, h][:], logs[b][:].indirect(picks(h * HALF, HALF)), ACT.Sigmoid, scale=-1.0)
 
-        def add_kick(b, h):
-            nc.vector.tensor_tensor(u2[b, h][:], kick[b][:].indirect(picks(h)), u1[b, h][:], ALU.add)
+        def fetch_cross(b, h, first=0, count=HALF):
+            cols = slice(first, first + count)
+            nc.vector.tensor_tensor(cross[b, h][:, cols], tw[b][:].indirect(picks(h * HALF + first, count)), vy[b, h][:, cols], ALU.mult)
 
-        def add_vx(b, h):
-            nc.vector.tensor_tensor(u3[b, h][:], u2[b, h][:], vx[b, h][:], ALU.add)
+        def fetch_kick(b, h, first=0, count=HALF):
+            cols = slice(first, first + count)
+            nc.vector.tensor_tensor(inner[b, h][:, cols], kick[b][:].indirect(picks(h * HALF + first, count)), cross[b, h][:, cols], ALU.add)
 
-        def rotate(b, h):
-            nc.vector.tensor_tensor(u4[b, h][:], u3[b, h][:], gain[b, h][:], ALU.mult)
+        def keep_vx(b, h):
+            nc.vector.scalar_tensor_tensor(kept[b, h][:], gain[b, h][:], 0.5, vx[b, h][:], ALU.subtract, ALU.mult)
 
-        def finish(b, h):
-            nc.vector.scalar_tensor_tensor(res[b, h][:], u4[b, h][:], 2.0, vx[b, h][:], ALU.mult, ALU.subtract)
-            nc.sync.dma_start(out=out[b * P : (b + 1) * P, cols_of(h)], in_=res[b, h][:])
+        def turn(b, h):
+            nc.vector.tensor_tensor(turned[b, h][:], inner[b, h][:], gain[b, h][:], ALU.mult)
 
-        cast_w("bz", 1, nc.vector.tensor_copy)
-        cast_w("ey", 0, nc.vector.tensor_copy)
-        for name, b in (("bz", 1), ("ey", 0)):
-            quant_w(name, b)
-            product(name, b)
-        cast_w("ex", 0)
+        def add_on_tensor(b, h, tag_flipped, tag_back):
+            flipped = psum.tile([P, HALF], F32, name=f"flipped{b}{h}", tag=tag_flipped)
+            for j in range(HALF // P):
+                cols = slice(j * P, (j + 1) * P)
+                nc.tensor.matmul(flipped[:, cols], lhsT=kept[b, h][:, cols], rhs=ident[:], is_transpose=True, start=True, stop=False)
+                nc.tensor.matmul(flipped[:, cols], lhsT=turned[b, h][:, cols], rhs=ident[:], is_transpose=True, start=False, stop=True)
+            staged = keep.tile([P, HALF], F32, name=f"staged{b}{h}")
+            nc.scalar.copy(staged[:], flipped[:])
+            back = psum.tile([P, HALF], F32, name=f"back{b}{h}", tag=tag_back)
+            for j in range(HALF // P):
+                cols = slice(j * P, (j + 1) * P)
+                nc.tensor.transpose(back[:, cols], staged[:, cols], ident[:])
+            nc.scalar.activation(res[b, h][:], back[:], ACT.Copy, scale=2.0)
+            nc.sync.dma_start(out=out[rows_of(b), h * HALF : (h + 1) * HALF], in_=res[b, h][:])
+
+        nc.vector.memset(planes[:].bitcast(I32), 0)
+        nc.vector.memset(one[:], 1.0)
+        nc.scalar.activation(warm[:], one[:], ACT.Ln)
+        for b in range(BLOCKS):
+            nc.vector.memset(tw[b][:, S:], 0.0)
+        make_identity(nc, ident[:])
+
+        load_w("bz")
+        nc.sync.dma_start(offs_t[:], offs)
+        for q in range(4):
+            nc.sync.dma_start(out=planes[32 * q : 32 * q + 4, :].bitcast(I32), in_=x_scales[0, 4 * q : 4 * q + 4, :].bitcast(I32))
+        nc.sync.dma_start(out=words[:], in_=x_words[0].rearrange("p c r -> p (c r)").bitcast(I32))
+        with nc.allow_non_contiguous_dma(reason="one value of qm for each partition and block"):
+            nc.sync.dma_start(out=qm_t[:], in_=qm.rearrange("(b p) o -> p (b o)", p=P))
+        nc.sync.dma_start(cell_t[:], cell)
+        load_w("ey")
+        load_vel(vy, vely, 0, 0)
+        load_w("ex")
+        load_vel(vy, vely, 0, 1)
+        load_vel(vy, vely, 1, 0)
+        load_vel(vx, velx, 0, 0)
+        load_vel(vx, velx, 0, 1)
+        load_vel(vx, velx, 1, 0)
+        load_vel(vy, vely, 1, 1)
+        load_vel(vx, velx, 1, 1)
+
+        nc.vector.tensor_copy(x_plane[:], planes[:].indirect(offs_t[:]))
+        for b in range(BLOCKS):
+            cast_w("bz", b, nc.scalar.copy)
+            quant_w("bz", b)
+        for c, bank in enumerate((acc["bz", 0], second_bank)):
+            nc.vector.tensor_copy(x_codes[c][:], words[:].bitcast(U32).indirect(offs_t[:, c * S // 32 : (c + 1) * S // 32]))
+            half_product(bank, "bz", 0, c)
+            nc.scalar.activation(tw[0][:, cells_of(c)], bank[:, cells_of(c)], ACT.Copy, scale=qm_t[:, 0:1])
+        product("bz", 1)
         nc.scalar.activation(tw[1][:, :S], acc["bz", 1][:], ACT.Copy, scale=qm_t[:, 1:2])
+
+        cast_w("ey", 0, nc.vector.tensor_copy)
+        quant_w("ey", 0)
+        product("ey", 0)
         for b in range(BLOCKS):
-            square(b)
+            nc.scalar.activation(logs[1 - b][:, S:], tw[b][:, :S], ACT.Square)
         for b in range(BLOCKS):
-            log_gain(b)
-        rotate_term(0, 0)
+            nc.scalar.activation(logs[b][:, :S], logs[1 - b][:, S:], ACT.Ln, bias=TINY)
+
+        fetch_cross(0, 0)
+        cast_w("ex", 0, nc.vector.tensor_copy)
+        kick_y(0)
         quant_w("ex", 0)
         product("ex", 0)
-        kick_y(0)
-        rotate_term(0, 1)
+        fetch_cross(0, 1)
         kick_x(0)
-        cast_w("ey", 1)
-        cast_w("ex", 1)
-        fetch_gain(0)
-        fetch_gain(1)
-        quant_w("ey", 1)
-        product("ey", 1)
-        add_kick(0, 0)
-        quant_w("ex", 1)
-        product("ex", 1)
-        add_kick(0, 1)
-        add_vx(0, 0)
+        cast_w("ey", 1, nc.scalar.copy)
+        cast_w("ex", 1, nc.scalar.copy)
+        for b, h in ((0, 0), (0, 1), (1, 0)):
+            fetch_gain(b, h)
+        fetch_kick(0, 0)
+        fetch_kick(0, 1)
+        for name in ("ey", "ex"):
+            quant_w(name, 1)
+            product(name, 1)
+        fetch_cross(1, 0)
         kick_y(1)
-        add_vx(0, 1)
+        keep_vx(0, 0)
         kick_x(1)
-        rotate(0, 0)
-        rotate(0, 1)
-        finish(0, 0)
-        finish(0, 1)
-        rotate_term(1, 0)
-        rotate_term(1, 1)
-        add_kick(1, 0)
-        add_kick(1, 1)
-        add_vx(1, 0)
-        add_vx(1, 1)
-        rotate(1, 0)
-        rotate(1, 1)
-        finish(1, 0)
-        finish(1, 1)
+        turn(0, 0)
+        keep_vx(0, 1)
+        turn(0, 1)
+        add_on_tensor(0, 0, "acc_bz0", "second_bank")
+        fetch_gain(1, 1)
+        fetch_kick(1, 0)
+        keep_vx(1, 0)
+        turn(1, 0)
+        add_on_tensor(0, 1, "acc_bz1", "last_bank")
+        add_on_tensor(1, 0, "acc_ey0", "acc_ex0")
+
+        quarter = HALF // 2
+        for first in (0, quarter):
+            fetch_cross(1, 1, first, quarter)
+        keep_vx(1, 1)
+        for first in (0, quarter):
+            fetch_kick(1, 1, first, quarter)
+        for first in (0, quarter):
+            cols = slice(first, first + quarter)
+            nc.vector.scalar_tensor_tensor(turned[1, 1][:, cols], inner[1, 1][:, cols], 2.0, gain[1, 1][:, cols], ALU.mult, ALU.mult)
+        for first in (0, quarter):
+            cols = slice(first, first + quarter)
+            nc.vector.scalar_tensor_tensor(res[1, 1][:, cols], kept[1, 1][:, cols], 2.0, turned[1, 1][:, cols], ALU.mult, ALU.add)
+            nc.sync.dma_start(out=out[rows_of(1), HALF + first : HALF + first + quarter], in_=res[1, 1][:, cols])

@@ -21,6 +21,7 @@ PACK = 4
 BLOCKS = N // P
 HALF = U // 2
 SPARE = 32
+EARLY = 768
 TINY = 2.0**-60
 
 
@@ -44,8 +45,8 @@ def tile_picked_yboris_vel_p_kernel(tc, x_words, x_scales, w1, w2, w3, qm, velx,
         weights = {"ex": w1, "ey": w2, "bz": w3}
         raw, grouped, codes, scales, acc = {}, {}, {}, {}, {}
         for name in weights:
-            raw[name] = keep.tile([P, PACK, N], F32, name=f"raw_{name}")
             for b in range(BLOCKS):
+                raw[name, b] = keep.tile([P, PACK, P], F32, name=f"raw_{name}{b}")
                 grouped[name, b] = keep.tile([P, P, PACK], BF16, name=f"grouped_{name}{b}", align_bytes=64)
                 codes[name, b] = keep.tile([P, P], U32, name=f"codes_{name}{b}", align_bytes=64)
                 scales[name, b] = keep.tile([P, P], U8, name=f"scales_{name}{b}", align_bytes=64)
@@ -78,8 +79,8 @@ def tile_picked_yboris_vel_p_kernel(tc, x_words, x_scales, w1, w2, w3, qm, velx,
         def picks(first, count):
             return cell_t[:, first // 16 : (first + count) // 16]
 
-        def load_w(name):
-            nc.sync.dma_start(out=raw[name][:], in_=weights[name].rearrange("(p j) m -> p j m", j=PACK))
+        def load_w(name, b):
+            nc.sync.dma_start(out=raw[name, b][:], in_=weights[name][:, rows_of(b)].rearrange("(p j) m -> p j m", j=PACK))
 
         def load_vel(tiles, src, b, h):
             nc.sync.dma_start(out=tiles[b, h][:], in_=src[rows_of(b), h * HALF : (h + 1) * HALF])
@@ -87,7 +88,7 @@ def tile_picked_yboris_vel_p_kernel(tc, x_words, x_scales, w1, w2, w3, qm, velx,
         def cast_w(name, b, copy):
             copy(
                 out=grouped[name, b][:].rearrange("p (c i) j -> p c j i", i=4),
-                in_=raw[name][:, :, rows_of(b)].rearrange("p j (c i) -> p c j i", i=4),
+                in_=raw[name, b][:].rearrange("p j (c i) -> p c j i", i=4),
             )
 
         def quant_w(name, b):
@@ -155,49 +156,55 @@ def tile_picked_yboris_vel_p_kernel(tc, x_words, x_scales, w1, w2, w3, qm, velx,
             nc.vector.memset(tw[b][:, S:], 0.0)
         make_identity(nc, ident[:])
 
-        load_w("bz")
+        table = x_words[0].rearrange("p c r -> p (c r)").bitcast(I32)
+        nc.sync.dma_start(out=words[:, :EARLY], in_=table[:, :EARLY])
         nc.sync.dma_start(offs_t[:], offs)
         for q in range(4):
             nc.sync.dma_start(out=planes[32 * q : 32 * q + 4, :].bitcast(I32), in_=x_scales[0, 4 * q : 4 * q + 4, :].bitcast(I32))
-        nc.sync.dma_start(out=words[:], in_=x_words[0].rearrange("p c r -> p (c r)").bitcast(I32))
+        nc.sync.dma_start(out=words[:, EARLY:], in_=table[:, EARLY:])
+        load_w("bz", 0)
         with nc.allow_non_contiguous_dma(reason="one value of qm for each partition and block"):
             nc.sync.dma_start(out=qm_t[:], in_=qm.rearrange("(b p) o -> p (b o)", p=P))
         nc.sync.dma_start(cell_t[:], cell)
-        load_w("ey")
+        load_w("bz", 1)
+        load_w("ey", 0)
+        load_w("ex", 0)
         load_vel(vy, vely, 0, 0)
-        load_w("ex")
         load_vel(vy, vely, 0, 1)
-        load_vel(vy, vely, 1, 0)
         load_vel(vx, velx, 0, 0)
         load_vel(vx, velx, 0, 1)
+        load_w("ey", 1)
+        load_w("ex", 1)
+        load_vel(vy, vely, 1, 0)
         load_vel(vx, velx, 1, 0)
         load_vel(vy, vely, 1, 1)
         load_vel(vx, velx, 1, 1)
 
         nc.vector.tensor_copy(x_plane[:], planes[:].indirect(offs_t[:]))
-        for b in range(BLOCKS):
-            cast_w("bz", b, nc.scalar.copy)
-            quant_w("bz", b)
-        for c, bank in enumerate((acc["bz", 0], second_bank)):
+        for c in range(2):
             nc.vector.tensor_copy(x_codes[c][:], words[:].bitcast(U32).indirect(offs_t[:, c * S // 32 : (c + 1) * S // 32]))
+        cast_w("bz", 0, nc.scalar.copy)
+        quant_w("bz", 0)
+        for c, bank in enumerate((acc["bz", 0], second_bank)):
             half_product(bank, "bz", 0, c)
             nc.scalar.activation(tw[0][:, cells_of(c)], bank[:, cells_of(c)], ACT.Copy, scale=qm_t[:, 0:1])
-        product("bz", 1)
-        nc.scalar.activation(tw[1][:, :S], acc["bz", 1][:], ACT.Copy, scale=qm_t[:, 1:2])
 
+        cast_w("bz", 1, nc.vector.tensor_copy)
         cast_w("ey", 0, nc.vector.tensor_copy)
+        quant_w("bz", 1)
+        cast_w("ex", 0, nc.vector.tensor_copy)
         quant_w("ey", 0)
-        product("ey", 0)
+        quant_w("ex", 0)
+        for name, b in (("bz", 1), ("ey", 0), ("ex", 0)):
+            product(name, b)
+        nc.scalar.activation(tw[1][:, :S], acc["bz", 1][:], ACT.Copy, scale=qm_t[:, 1:2])
         for b in range(BLOCKS):
             nc.scalar.activation(logs[1 - b][:, S:], tw[b][:, :S], ACT.Square)
         for b in range(BLOCKS):
             nc.scalar.activation(logs[b][:, :S], logs[1 - b][:, S:], ACT.Ln, bias=TINY)
 
         fetch_cross(0, 0)
-        cast_w("ex", 0, nc.vector.tensor_copy)
         kick_y(0)
-        quant_w("ex", 0)
-        product("ex", 0)
         fetch_cross(0, 1)
         kick_x(0)
         cast_w("ey", 1, nc.scalar.copy)

from contextlib import ExitStack

import concourse.mybir as mybir
from concourse.masks import make_identity

K, T, S, N, U = 512, 2048, 512, 256, 1024
FLOPS = 3 * 2 * K * N * S

F32 = mybir.dt.float32
BF16 = mybir.dt.bfloat16
I32 = mybir.dt.int32
U32 = mybir.dt.uint32
U16 = mybir.dt.uint16
U8 = mybir.dt.uint8
FP8X4 = mybir.dt.float8_e4m3fn_x4
ALU = mybir.AluOpType
ACT = mybir.ActivationFunctionType

P = 128
PACK = 4
BLOCKS = N // P
HALF = U // 2
SPARE = 32
EARLY = 768
TINY = 2.0**-60


def tile_picked_yboris_vel_p_kernel(tc, x_words, x_scales, w1, w2, w3, qm, velx, vely, offs, cell, out):
    nc = tc.nc
    with ExitStack() as ctx:
        keep = ctx.enter_context(tc.tile_pool(name="keep", bufs=1))
        psum = ctx.enter_context(tc.psum_pool(name="psum", bufs=1))

        offs_t = keep.tile([P, S // 16], U16, name="offs_t")
        cell_t = keep.tile([P, U // 16], U16, name="cell_t")
        words = keep.tile([P, T], I32, name="words", align_bytes=64)
        planes = keep.tile([P, T], U8, name="planes", align_bytes=64)
        x_codes = [keep.tile([P, S // 2], U32, name=f"x_codes{c}", align_bytes=64) for c in range(2)]
        x_plane = keep.tile([P, S], U8, name="x_plane", align_bytes=64)
        qm_t = keep.tile([P, BLOCKS], F32, name="qm_t")
        one = keep.tile([P, 8], F32, name="one")
        warm = keep.tile([P, 8], F32, name="warm")
        ident = keep.tile([P, P], F32, name="ident")

        weights = {"ex": w1, "ey": w2, "bz": w3}
        raw, grouped, codes, scales, acc = {}, {}, {}, {}, {}
        for name in weights:
            for b in range(BLOCKS):
                raw[name, b] = keep.tile([P, PACK, P], F32, name=f"raw_{name}{b}")
                grouped[name, b] = keep.tile([P, P, PACK], BF16, name=f"grouped_{name}{b}", align_bytes=64)
                codes[name, b] = keep.tile([P, P], U32, name=f"codes_{name}{b}", align_bytes=64)
                scales[name, b] = keep.tile([P, P], U8, name=f"scales_{name}{b}", align_bytes=64)
                acc[name, b] = psum.tile([P, S], F32, name=f"acc_{name}{b}", tag=f"acc_{name}{b}")
        second_bank = psum.tile([P, S], F32, name="second_bank", tag="second_bank")

        def per_block(name, width):
            return [keep.tile([P, width], F32, name=f"{name}{b}") for b in range(BLOCKS)]

        def per_half(name, skip=()):
            return {
                (b, h): keep.tile([P, HALF], F32, name=f"{name}{b}{h}") for b in range(BLOCKS) for h in range(2) if (b, h) not in skip
            }

        vx, vy = per_half("vx"), per_half("vy")
        tw, kick, logs = per_block("tw", S + SPARE), per_block("kick", 2 * S), per_block("logs", 2 * S)
        cross, inner, gain = per_half("cross", [(1, 0), (1, 1)]), per_half("inner", [(1, 0)]), per_half("gain", [(1, 1)])
        kept, turned, res = per_half("kept"), per_half("turned"), per_half("res")
        cross[1, 0] = cross[0, 1]
        inner[1, 0] = inner[0, 1]
        cross[1, 1] = inner[1, 0]
        gain[1, 1] = gain[0, 0]

        def rows_of(b):
            return slice(b * P, (b + 1) * P)

        def cells_of(c):
            return slice(c * S // 2, (c + 1) * S // 2)

        def picks(first, count):
            return cell_t[:, first // 16 : (first + count) // 16]

        def load_w(name, b):
            nc.sync.dma_start(out=raw[name, b][:], in_=weights[name][:, rows_of(b)].rearrange("(p j) m -> p j m", j=PACK))

        def load_vel(tiles, src, b, h):
            nc.sync.dma_start(out=tiles[b, h][:], in_=src[rows_of(b), h * HALF : (h + 1) * HALF])

        def cast_w(name, b, copy):
            copy(
                out=grouped[name, b][:].rearrange("p (c i) j -> p c j i", i=4),
                in_=raw[name, b][:].rearrange("p j (c i) -> p c j i", i=4),
            )

        def quant_w(name, b):
            nc.vector.quantize_mx(
                out=codes[name, b][:].bitcast(FP8X4), scales=scales[name, b][:], in_=grouped[name, b][:].rearrange("p m j -> p (m j)")
            )

        def half_product(bank, name, b, c):
            nc.tensor.matmul_mx(
                out=bank[:, cells_of(c)],
                lhsT=codes[name, b][:].bitcast(FP8X4),
                lhsT_scale=scales[name, b][:],
                rhs=x_codes[c][:].bitcast(FP8X4),
                rhs_scale=x_plane[:, cells_of(c)],
                start=True,
                stop=True,
            )

        def product(name, b):
            for c in range(2):
                half_product(acc[name, b], name, b, c)

        def kick_y(b):
            nc.vector.scalar_tensor_tensor(kick[b][:, S:], acc["ey", b][:], qm_t[:, b : b + 1], tw[b][:, :S], ALU.mult, ALU.mult)

        def kick_x(b):
            nc.vector.scalar_tensor_tensor(kick[b][:, :S], acc["ex", b][:], qm_t[:, b : b + 1], kick[b][:, S:], ALU.mult, ALU.add)

        def fetch_gain(b, h):
            nc.scalar.activation(gain[b, h][:], logs[b][:].indirect(picks(h * HALF, HALF)), ACT.Sigmoid, scale=-1.0)

        def fetch_cross(b, h, first=0, count=HALF):
            cols = slice(first, first + count)
            nc.vector.tensor_tensor(cross[b, h][:, cols], tw[b][:].indirect(picks(h * HALF + first, count)), vy[b, h][:, cols], ALU.mult)

        def fetch_kick(b, h, first=0, count=HALF):
            cols = slice(first, first + count)
            nc.vector.tensor_tensor(inner[b, h][:, cols], kick[b][:].indirect(picks(h * HALF + first, count)), cross[b, h][:, cols], ALU.add)

        def keep_vx(b, h):
            nc.vector.scalar_tensor_tensor(kept[b, h][:], gain[b, h][:], 0.5, vx[b, h][:], ALU.subtract, ALU.mult)

        def turn(b, h):
            nc.vector.tensor_tensor(turned[b, h][:], inner[b, h][:], gain[b, h][:], ALU.mult)

        def add_on_tensor(b, h, tag_flipped, tag_back):
            flipped = psum.tile([P, HALF], F32, name=f"flipped{b}{h}", tag=tag_flipped)
            for j in range(HALF // P):
                cols = slice(j * P, (j + 1) * P)
                nc.tensor.matmul(flipped[:, cols], lhsT=kept[b, h][:, cols], rhs=ident[:], is_transpose=True, start=True, stop=False)
                nc.tensor.matmul(flipped[:, cols], lhsT=turned[b, h][:, cols], rhs=ident[:], is_transpose=True, start=False, stop=True)
            staged = keep.tile([P, HALF], F32, name=f"staged{b}{h}")
            nc.scalar.copy(staged[:], flipped[:])
            back = psum.tile([P, HALF], F32, name=f"back{b}{h}", tag=tag_back)
            for j in range(HALF // P):
                cols = slice(j * P, (j + 1) * P)
                nc.tensor.transpose(back[:, cols], staged[:, cols], ident[:])
            nc.scalar.activation(res[b, h][:], back[:], ACT.Copy, scale=2.0)
            nc.sync.dma_start(out=out[rows_of(b), h * HALF : (h + 1) * HALF], in_=res[b, h][:])

        nc.vector.memset(planes[:].bitcast(I32), 0)
        nc.vector.memset(one[:], 1.0)
        nc.scalar.activation(warm[:], one[:], ACT.Ln)
        for b in range(BLOCKS):
            nc.vector.memset(tw[b][:, S:], 0.0)
        make_identity(nc, ident[:])

        table = x_words[0].rearrange("p c r -> p (c r)").bitcast(I32)
        nc.sync.dma_start(out=words[:, :EARLY], in_=table[:, :EARLY])
        nc.sync.dma_start(offs_t[:], offs)
        for q in range(4):
            nc.sync.dma_start(out=planes[32 * q : 32 * q + 4, :].bitcast(I32), in_=x_scales[0, 4 * q : 4 * q + 4, :].bitcast(I32))
        nc.sync.dma_start(out=words[:, EARLY:], in_=table[:, EARLY:])
        load_w("bz", 0)
        with nc.allow_non_contiguous_dma(reason="one value of qm for each partition and block"):
            nc.sync.dma_start(out=qm_t[:], in_=qm.rearrange("(b p) o -> p (b o)", p=P))
        nc.sync.dma_start(cell_t[:], cell)
        load_w("bz", 1)
        load_w("ey", 0)
        load_w("ex", 0)
        load_vel(vy, vely, 0, 0)
        load_vel(vy, vely, 0, 1)
        load_vel(vx, velx, 0, 0)
        load_vel(vx, velx, 0, 1)
        load_w("ey", 1)
        load_w("ex", 1)
        load_vel(vy, vely, 1, 0)
        load_vel(vx, velx, 1, 0)
        load_vel(vy, vely, 1, 1)
        load_vel(vx, velx, 1, 1)

        nc.vector.tensor_copy(x_plane[:], planes[:].indirect(offs_t[:]))
        for c in range(2):
            nc.vector.tensor_copy(x_codes[c][:], words[:].bitcast(U32).indirect(offs_t[:, c * S // 32 : (c + 1) * S // 32]))
        cast_w("bz", 0, nc.scalar.copy)
        quant_w("bz", 0)
        for c, bank in enumerate((acc["bz", 0], second_bank)):
            half_product(bank, "bz", 0, c)
            nc.scalar.activation(tw[0][:, cells_of(c)], bank[:, cells_of(c)], ACT.Copy, scale=qm_t[:, 0:1])

        cast_w("bz", 1, nc.vector.tensor_copy)
        cast_w("ey", 0, nc.vector.tensor_copy)
        quant_w("bz", 1)
        cast_w("ex", 0, nc.vector.tensor_copy)
        quant_w("ey", 0)
        quant_w("ex", 0)
        for name, b in (("bz", 1), ("ey", 0), ("ex", 0)):
            product(name, b)
        nc.scalar.activation(tw[1][:, :S], acc["bz", 1][:], ACT.Copy, scale=qm_t[:, 1:2])
        for b in range(BLOCKS):
            nc.scalar.activation(logs[1 - b][:, S:], tw[b][:, :S], ACT.Square)
        for b in range(BLOCKS):
            nc.scalar.activation(logs[b][:, :S], logs[1 - b][:, S:], ACT.Ln, bias=TINY)

        fetch_cross(0, 0)
        kick_y(0)
        fetch_cross(0, 1)
        kick_x(0)
        cast_w("ey", 1, nc.scalar.copy)
        cast_w("ex", 1, nc.scalar.copy)
        for b, h in ((0, 0), (0, 1), (1, 0)):
            fetch_gain(b, h)
        fetch_kick(0, 0)
        fetch_kick(0, 1)
        for name in ("ey", "ex"):
            quant_w(name, 1)
            product(name, 1)
        fetch_cross(1, 0)
        kick_y(1)
        keep_vx(0, 0)
        kick_x(1)
        turn(0, 0)
        keep_vx(0, 1)
        turn(0, 1)
        add_on_tensor(0, 0, "acc_bz0", "second_bank")
        fetch_gain(1, 1)
        fetch_kick(1, 0)
        keep_vx(1, 0)
        turn(1, 0)
        add_on_tensor(0, 1, "acc_bz1", "last_bank")
        add_on_tensor(1, 0, "acc_ey0", "acc_ex0")

        quarter = HALF // 2
        for first in (0, quarter):
            fetch_cross(1, 1, first, quarter)
        keep_vx(1, 1)
        for first in (0, quarter):
            fetch_kick(1, 1, first, quarter)
        for first in (0, quarter):
            cols = slice(first, first + quarter)
            nc.vector.scalar_tensor_tensor(turned[1, 1][:, cols], inner[1, 1][:, cols], 2.0, gain[1, 1][:, cols], ALU.mult, ALU.mult)
        for first in (0, quarter):
            cols = slice(first, first + quarter)
            nc.vector.scalar_tensor_tensor(res[1, 1][:, cols], kept[1, 1][:, cols], 2.0, turned[1, 1][:, cols], ALU.mult, ALU.add)
            nc.sync.dma_start(out=out[rows_of(1), HALF + first : HALF + first + quarter], in_=res[1, 1][:, cols])
